import numpy as np
import ml_dtypes


def mxq(x, axis, fmt="e4m3"):
    dtype, down = {"e4m3": (ml_dtypes.float8_e4m3fn, 7), "e5m2": (ml_dtypes.float8_e5m2, 14)}[fmt]
    v = np.moveaxis(np.asarray(x, np.float32).astype(ml_dtypes.bfloat16).astype(np.float64), axis, -1)
    blocks = v.reshape(v.shape[:-1] + (-1, 32))
    amax = np.abs(blocks).max(-1, keepdims=True)
    byte = np.maximum(np.where(amax > 0, np.frexp(amax)[1] - 1 + 127, 0) - down, 1)
    scale = np.exp2(byte - 127.0)
    codes = (blocks / scale).astype(np.float32).astype(dtype).astype(np.float64)
    return np.moveaxis((codes * scale).reshape(v.shape), -1, axis)


WIDE = False


def mx_kscale(k):
    if not WIDE:
        return np.ones(k)
    levels = np.array([10, -10, 5, -5, 0])
    if k % 512:
        return np.exp2(np.random.permutation(np.resize(levels, k // 32))).repeat(32)
    a = np.empty((k // 512, 16))
    for p in range(k // 512):
        a[p, :8] = np.random.permutation(np.resize(levels, 8))
        for g in range(8):
            far = levels[np.abs(levels - a[p, g]) >= 10]
            a[p, g + 8] = far[np.random.randint(len(far))]
    return np.exp2(a.ravel()).repeat(32)


def f64(x):
    return np.asarray(x).astype(np.float64)


def striped(idx):
    return np.tile(idx.reshape(-1, 16).T, (8, 1)).astype(np.uint16)


def unstriped(offs):
    return offs[:16].T.reshape(-1).astype(np.int64)


def striped8(idx):
    return np.concatenate([x.reshape(-1, 16).T for x in idx]).astype(np.uint16)


def runs(offs, k):
    lists = np.stack([offs[16 * r : 16 * r + 16].T.reshape(-1) for r in range(8)]).astype(np.int64)
    return lists[np.arange(k) % 512 // 64]


def pack_weight(w):
    k, n = w.shape
    w = f64(np.asarray(w, np.float32).astype(ml_dtypes.bfloat16)).reshape(k // 32, 32, n)
    amax = np.abs(w).max(1)
    byte = np.clip(np.where(amax > 0, np.frexp(amax)[1] - 1 + 127 - 7, 1), 1, 254)
    scaled = (w * np.exp2(127.0 - byte)[:, None, :]).reshape(k, n).astype(np.float32)
    words = np.ascontiguousarray(scaled.reshape(k // 512, 128, 4, n).transpose(0, 1, 3, 2)).astype(ml_dtypes.float8_e4m3fn).view(np.uint8)
    return words, np.ascontiguousarray(byte.astype(np.uint8).reshape(k // 512, 16, n))


def unpack_weight(words, scales):
    g, p, n, _ = words.shape
    vals = np.ascontiguousarray(words).view(ml_dtypes.float8_e4m3fn).astype(np.float64) * np.repeat(np.exp2(scales.astype(np.float64) - 127.0), 8, axis=1)[..., None]
    return vals.transpose(0, 1, 3, 2).reshape(g * 512, n)


E2M1 = np.array([0.0, 0.5, 1.0, 1.5, 2.0, 3.0, 4.0, 6.0, -0.0, -0.5, -1.0, -1.5, -2.0, -3.0, -4.0, -6.0])


def pack_fp4(w):
    k, n = w.shape
    w = f64(np.asarray(w, np.float32).astype(ml_dtypes.bfloat16)).reshape(k // 32, 32, n)
    amax = np.abs(w).max(1)
    mant, ex = np.frexp(amax / 6.0)
    byte = np.clip(np.where(amax > 0, np.where(mant > 0.5, ex, ex - 1) + 127, 1), 1, 254)
    scaled = (w * np.exp2(127.0 - byte)[:, None, :]).reshape(k, n).astype(np.float32)
    c = np.ascontiguousarray(scaled.reshape(k // 512, 128, 4, n).transpose(0, 1, 3, 2)).astype(ml_dtypes.float4_e2m1fn).view(np.uint8) & 0xF
    words = (c[..., 0::2] | (c[..., 1::2] << 4)).reshape(k // 512, 128, 2 * n)
    return np.ascontiguousarray(words), np.ascontiguousarray(byte.astype(np.uint8).reshape(k // 512, 16, n))


def unpack_fp4(words, scales):
    g, _, n = scales.shape
    words = np.ascontiguousarray(words).reshape(g, 128, n, 2)
    nib = np.empty((g, 128, n, 4), np.uint8)
    nib[..., 0::2] = words & 0xF
    nib[..., 1::2] = words >> 4
    vals = E2M1[nib] * np.repeat(np.exp2(scales.astype(np.float64) - 127.0), 8, axis=1)[..., None]
    return vals.transpose(0, 1, 3, 2).reshape(g * 512, n)


def planes(y):
    n, m = y.shape
    v = y.astype(np.float32).astype(ml_dtypes.bfloat16).astype(np.float64).reshape(n // 32, 32, m)
    top = np.abs(v).max(1)
    byte = np.clip(np.where(top > 0, np.frexp(top)[1] - 1 + 127 - 7, 1), 1, 254)
    codes = (v * np.exp2(127.0 - byte)[:, None, :]).reshape(n, m).astype(np.float32).astype(ml_dtypes.float8_e4m3fn).view(np.uint8)
    words = codes.reshape(n // 512, 128, 4, m).transpose(0, 1, 3, 2)
    return np.ascontiguousarray(words), np.ascontiguousarray(byte.astype(np.uint8).reshape(n // 512, 16, m))


K, T, S, N, H, U = 512, 2048, 512, 512, 512, 1024
P = 2 ** 7


def setup_inputs():
    n = np.random.standard_normal
    s = mx_kscale(K)[:, None]
    u = mx_kscale(H)
    packed_xT = pack_weight(n((K, T)) * s)
    packed_w1 = pack_fp4(n((K, H)) / np.sqrt(K) / s)
    packed_w2 = pack_fp4(n((K, H)) / np.sqrt(K) / s)
    packed_w3 = pack_fp4(n((H, N)) / np.sqrt(H) / u[:, None])
    return {
        "x_words": packed_xT[0],
        "x_scales": packed_xT[1],
        "w1_words": packed_w1[0],
        "w1_scales": packed_w1[1],
        "w2_words": packed_w2[0],
        "w2_scales": packed_w2[1],
        "best": n((H, S)).astype(np.float32),
        "ra": np.tile(np.random.uniform(0.3, 1.0, S), (P, 1)).astype(np.float32),
        "rb": np.tile(np.random.uniform(0.3, 1.0, S), (P, 1)).astype(np.float32),
        "gn": (np.random.uniform(0.5, 1.5, (H, 1)) * u[:, None]).astype(np.float32),
        "w3_words": packed_w3[0],
        "w3_scales": packed_w3[1],
        "mem": n((N, U)).astype(np.float32),
        "offs": striped(np.random.permutation(T)[:S]),
        "two": striped(np.random.permutation(T)[:S]),
        "n1": striped8(np.stack([np.random.permutation(S) for _ in range(8)])),
        "n2": striped8(np.stack([np.random.permutation(S) for _ in range(8)])),
        "slot": striped8(np.stack([np.random.permutation(U)[:S] for _ in range(8)])),
    }


def reference(x_words, x_scales, w1_words, w1_scales, w2_words, w2_scales, best, ra, rb, gn, w3_words, w3_scales, mem, offs, two, n1, n2, slot):
    x_two = unpack_weight(x_words, x_scales)[:, unstriped(two)]
    c = unpack_fp4(w2_words, w2_scales).T @ x_two
    xq = unpack_weight(x_words, x_scales)[:, unstriped(offs)]
    y = unpack_fp4(w1_words, w1_scales).T @ xq
    z = f64(gn) * (0.75 * c + f64(ra)[:1] * (f64(best) - y) + f64(rb)[:1] * (np.maximum(f64(best)[np.arange(H)[:, None], runs(n1, H)], f64(best)[np.arange(H)[:, None], runs(n2, H)]) - y))
    h = unpack_fp4(w3_words, w3_scales).T @ mxq(z, 0, "e4m3")
    out = f64(mem).copy()
    out[np.arange(N)[:, None], runs(slot, N)] = h
    return (out,) + planes(out)

@@ -1,0 +1,267 @@
+from contextlib import ExitStack
+
+import concourse.mybir as mybir
+from concourse.masks import make_identity
+
+K, T, S, N, H, U = 512, 2048, 512, 512, 512, 1024
+FLOPS = 3 * 2 * 512 * 512 * 512
+
+F32 = mybir.dt.float32
+BF16 = mybir.dt.bfloat16
+I32 = mybir.dt.int32
+U32 = mybir.dt.uint32
+U16 = mybir.dt.uint16
+U8 = mybir.dt.uint8
+FP8X4 = mybir.dt.float8_e4m3fn_x4
+FP4X4 = mybir.dt.float4_e2m1fn_x4
+COPY = mybir.ActivationFunctionType.Copy
+ALU = mybir.AluOpType
+
+P = 128
+PACK = 4
+HALF = S // 2
+LIST_COLS = HALF // 16
+CHUNK = U // 2
+
+
+def tile_picked_swarm2_none_po_kernel(
+    tc, x_words, x_scales, w1_words, w1_scales, w2_words, w2_scales, best, ra, rb, gn,
+    w3_words, w3_scales, mem, offs, two, n1, n2, slot, out_0, out_1, out_2,
+):
+    nc = tc.nc
+    with ExitStack() as ctx:
+        lists = ctx.enter_context(tc.tile_pool(name="lists", bufs=1))
+        sb = ctx.enter_context(tc.tile_pool(name="sb", bufs=1))
+        acc = ctx.enter_context(tc.psum_pool(name="acc", bufs=1))
+        ring = ctx.enter_context(tc.psum_pool(name="ring", bufs=4))
+
+        def tile(shape, dtype, name, tag=None):
+            return sb.tile(shape, dtype, name=name, tag=tag or name, align_bytes=64)
+
+        def load_list(src, name):
+            dst = lists.tile([P, S // 16], U16, name=name)
+            nc.sync.dma_start(dst[:], src)
+            return dst
+
+        def load_scales(queue, dst, src):
+            for q in range(4):
+                queue.dma_start(dst[32 * q : 32 * q + 4, :].bitcast(I32), src[0, 4 * q : 4 * q + 4, :].bitcast(I32))
+
+        def half_of(lst, half):
+            return lst[:, half * LIST_COLS : (half + 1) * LIST_COLS]
+
+        pulls_rows = tile([P, P], F32, "pulls_rows")
+        nc.vector.memset(pulls_rows[:], 0.0)
+        xs = tile([P, T], U8, "xs")
+        w1s = tile([P, H], U8, "w1s")
+        w2s = tile([P, H], U8, "w2s")
+        w3s = tile([P, N], U8, "w3s")
+        for plane in (xs, w2s, w1s, w3s):
+            nc.vector.memset(plane[:].bitcast(I32), 0)
+        ident = tile([P, P], F32, "ident")
+        make_identity(nc, ident[:])
+
+        best_rows = best.rearrange("(p t) j -> t p j", t=PACK)
+        mem_rows = mem.rearrange("(p t) c -> t p c", t=PACK)
+        out_rows = out_0.rearrange("(p t) c -> t p c", t=PACK)
+        bt = [tile([P, S], F32, f"best{t}") for t in range(PACK)]
+        n1_l = load_list(n1, "n1_l")
+        nc.sync.dma_start(bt[0][:], best_rows[0])
+        n2_l = load_list(n2, "n2_l")
+        for t in range(1, PACK):
+            nc.sync.dma_start(bt[t][:], best_rows[t])
+        xw = tile([P, T], I32, "xw")
+        nc.sync.dma_start(xw[:], x_words[0].rearrange("p n t -> p (n t)").bitcast(I32))
+        two_l = load_list(two, "two_l")
+        offs_l = load_list(offs, "offs_l")
+        nc.scalar.dma_start(pulls_rows[0:4, :], ra[0:1, :].rearrange("o (b c) -> (o b) c", b=4))
+        nc.scalar.dma_start(pulls_rows[4:8, :], rb[0:1, :].rearrange("o (b c) -> (o b) c", b=4))
+        load_scales(nc.scalar, xs, x_scales)
+        w1w = tile([P, 2 * H], U8, "w1w")
+        w2w = tile([P, 2 * H], U8, "w2w")
+        w3w = tile([P, 2 * N], U8, "w3w")
+        nc.sync.dma_start(w2w[:].bitcast(I32), w2_words[0].bitcast(I32))
+        nc.sync.dma_start(w1w[:].bitcast(I32), w1_words[0].bitcast(I32))
+        load_scales(nc.scalar, w2s, w2_scales)
+        load_scales(nc.scalar, w1s, w1_scales)
+        gain = tile([P, PACK], F32, "gain")
+        nc.sync.dma_start(gain[:], gn.rearrange("(p t) o -> p (t o)", t=PACK))
+        nc.sync.dma_start(w3w[:].bitcast(I32), w3_words[0].bitcast(I32))
+        load_scales(nc.sync, w3s, w3_scales)
+        slot_l = load_list(slot, "slot_l")
+        page = [tile([P, U], F32, f"page{t}") for t in range(PACK)]
+        for t in range(PACK):
+            nc.sync.dma_start(page[t][:], mem_rows[t])
+
+        pulls_ps = ring.tile([P, S], F32, name="pulls_ps", tag="ring")
+        nc.tensor.transpose(pulls_ps[:, 0:P], pulls_rows[:], ident[:])
+        pulls = tile([P, 8], F32, "pulls")
+        nc.scalar.copy(pulls[:], pulls_ps[:, 0:8])
+        neg_sum = tile([P, 4], F32, "neg_sum")
+        nc.vector.scalar_tensor_tensor(neg_sum[:], pulls[:, 0:4], -1.0, pulls[:, 4:8], ALU.mult, ALU.subtract)
+
+        zsum = [[acc.tile([P, 2, HALF], F32, name=f"zsum{h}{u}", tag=f"z{h}{u}") for u in range(2)] for h in range(2)]
+        added = {}
+
+        def add_term(term, jb, t):
+            h, u = jb // 2, t // 2
+            count = added.get((h, u), 0)
+            added[(h, u)] = count + 1
+            c0 = (jb % 2) * P
+            nc.tensor.matmul(zsum[h][u][:, t % 2, c0 : c0 + P], term, ident[:], start=(count == 0), stop=(count == 15), is_transpose=True)
+
+        def neighbour_gathers(half, t, tag):
+            pair = tile([P, 2, HALF], F32, f"pair{half}{t}", tag)
+            nc.vector.tensor_copy(pair[:, 0, :], bt[t][:].indirect(half_of(n1_l, half)))
+            nc.vector.tensor_copy(pair[:, 1, :], bt[t][:].indirect(half_of(n2_l, half)))
+            return pair
+
+        def neighbour_max(half, t, pair):
+            top = tile([P, HALF], F32, f"top{half}{t}")
+            nc.vector.tensor_tensor(top[:], pair[:, 0, :], pair[:, 1, :], ALU.max)
+            return top
+
+        def neighbour_term(half, t, top, pool, tag):
+            ps = pool.tile([P, 2, HALF], F32, name=f"topT{half}{t}", tag=tag)
+            term = tile([P, 2, P], F32, f"top_term{half}{t}")
+            for b in range(2):
+                nc.tensor.transpose(ps[:, 0, b * P : (b + 1) * P], top[:, b * P : (b + 1) * P], ident[:])
+            for b in range(2):
+                jb = 2 * half + b
+                nc.scalar.activation(term[:, b, :], ps[:, 0, b * P : (b + 1) * P], COPY, scale=pulls[:, 4 + jb : 5 + jb])
+            for b in range(2):
+                add_term(term[:, b, :], 2 * half + b, t)
+
+        def best_term(jb):
+            ps = ring.tile([P, S], F32, name=f"bestT{jb}", tag="ring")
+            for t in range(PACK):
+                nc.tensor.transpose(ps[:, t * P : (t + 1) * P], bt[t][:, jb * P : (jb + 1) * P], ident[:])
+            term = tile([P, PACK, P], F32, f"best_term{jb}")
+            nc.scalar.activation(term[:].rearrange("j t p -> j (t p)"), ps[:], COPY, scale=pulls[:, jb : jb + 1])
+            for t in range(PACK):
+                add_term(term[:, t, :], jb, t)
+
+        def pick(lst, name, half):
+            words = tile([P, HALF], I32, f"{name}_words{half}")
+            scales = tile([P, HALF], U8, f"{name}_scales{half}")
+            nc.vector.tensor_copy(words[:].bitcast(U32), xw[:].bitcast(U32).indirect(half_of(lst, half)))
+            nc.vector.tensor_copy(scales[:], xs[:].indirect(half_of(lst, half)))
+            return words, scales
+
+        def product_term(picked, ww, ws, name, jb, scale):
+            words, scales = picked
+            cols = slice((jb % 2) * P, (jb % 2 + 1) * P)
+            ps = ring.tile([P, S], F32, name=f"{name}T{jb}", tag="ring")
+            nc.tensor.matmul_mx(ps[:], lhsT=words[:, cols].bitcast(FP8X4), lhsT_scale=scales[:, cols],
+                                rhs=ww[:].bitcast(FP4X4), rhs_scale=ws[:], start=True, stop=True)
+            term = tile([P, PACK, P], F32, f"{name}_term{jb}")
+            nc.scalar.activation(term[:], ps[:].rearrange("j (p t) -> j t p", t=PACK), COPY, scale=scale)
+            for t in range(PACK):
+                add_term(term[:, t, :], jb, t)
+
+        def product_terms(half, picked_two, picked_offs):
+            for jb in (2 * half, 2 * half + 1):
+                product_term(picked_two, w2w, w2s, "c", jb, 0.75)
+            for jb in (2 * half, 2 * half + 1):
+                product_term(picked_offs, w1w, w1s, "y", jb, neg_sum[:, jb : jb + 1])
+
+        def round_z(half):
+            planes = tile([P, PACK, HALF], BF16, f"z_planes{half}")
+            for t in range(PACK):
+                nc.scalar.activation(planes[:, t, :], zsum[half][t // 2][:, t % 2, :], COPY, scale=gain[:, t : t + 1])
+            grouped = tile([P, HALF, PACK], BF16, f"z_grouped{half}")
+            nc.scalar.copy(grouped[:].rearrange("p (c i) t -> p c t i", i=4), planes[:].rearrange("p t (c i) -> p c t i", i=4))
+            return grouped
+
+        def quantize_z(half, grouped):
+            words = tile([P, HALF], I32, f"z_words{half}")
+            scales = tile([P, HALF], U8, f"z_scales{half}")
+            nc.vector.quantize_mx(words[:].bitcast(FP8X4), scales[:], grouped[:].rearrange("p c t -> p (c t)"))
+            return words, scales
+
+        def layer(half, quantized):
+            words, scales = quantized
+            banks = []
+            for u in range(2):
+                ps = ring.tile([P, S], F32, name=f"h{half}{u}", tag="ring")
+                for t in (2 * u, 2 * u + 1):
+                    nc.tensor.matmul_mx(ps[:, (t % 2) * HALF : (t % 2 + 1) * HALF],
+                                        lhsT=w3w_d[:, t * 2 * P : (t + 1) * 2 * P].bitcast(FP4X4), lhsT_scale=w3s_d[:, t * P : (t + 1) * P],
+                                        rhs=words[:].bitcast(FP8X4), rhs_scale=scales[:], start=True, stop=True)
+                banks.append(ps)
+            return banks
+
+        def copy_h(half, t, banks, tag=None):
+            vals = tile([P, HALF], F32, f"h_vals{half}{t}", tag)
+            nc.scalar.copy(vals[:], banks[t // 2][:, (t % 2) * HALF : (t % 2 + 1) * HALF])
+            return vals
+
+        def scatter(half, t, vals):
+            nc.vector.tensor_copy(page[t][:].indirect(half_of(slot_l, half)), vals[:])
+
+        tops = []
+        pairs = [neighbour_gathers(0, 0, "pair00")]
+        for t in range(1, PACK):
+            pairs.append(neighbour_gathers(0, t, f"pair0{t}"))
+            tops.append(neighbour_max(0, t - 1, pairs[t - 1]))
+        two_a = pick(two_l, "two", 0)
+        tops.append(neighbour_max(0, PACK - 1, pairs[PACK - 1]))
+        offs_a = pick(offs_l, "offs", 0)
+        for jb in range(2):
+            best_term(jb)
+        for t in range(PACK):
+            neighbour_term(0, t, tops[t], ring, "ring")
+        product_terms(0, two_a, offs_a)
+        grouped_a = round_z(0)
+
+        w3w_d = tile([P, 2 * N], U8, "w3w_d")
+        w3s_d = tile([P, N], U8, "w3s_d")
+        nc.vector.tensor_copy(w3w_d[:].rearrange("k (t m b) -> k t m b", t=PACK, b=2), w3w[:].rearrange("k (m t b) -> k t m b", t=PACK, b=2))
+        nc.vector.tensor_copy(w3s_d[:].rearrange("k (t m) -> k t m", t=PACK), w3s[:].rearrange("k (m t) -> k t m", t=PACK))
+
+        two_b = pick(two_l, "two", 1)
+        offs_b = pick(offs_l, "offs", 1)
+        for jb in range(2, 4):
+            best_term(jb)
+        product_terms(1, two_b, offs_b)
+        pair0 = neighbour_gathers(1, 0, "two_words0")
+        pair1 = neighbour_gathers(1, 1, "offs_words0")
+        top0 = neighbour_max(1, 0, pair0)
+        pair2 = neighbour_gathers(1, 2, "two_words0")
+        top1 = neighbour_max(1, 1, pair1)
+        quant_a = quantize_z(0, grouped_a)
+        top2 = neighbour_max(1, 2, pair2)
+        for t, top in enumerate((top0, top1, top2)):
+            neighbour_term(1, t, top, acc, f"z0{t % 2}")
+        banks_a = layer(0, quant_a)
+        pair3 = neighbour_gathers(1, 3, "z_grouped0")
+        top3 = neighbour_max(1, 3, pair3)
+        vals_a = [copy_h(0, 0, banks_a)]
+        neighbour_term(1, 3, top3, acc, "z01")
+        grouped_b = round_z(1)
+        vals_a.extend(copy_h(0, t, banks_a) for t in (1, 2))
+        for t in range(3):
+            scatter(0, t, vals_a[t])
+        quant_b = quantize_z(1, grouped_b)
+        scatter(0, 3, copy_h(0, 3, banks_a, "z_grouped1"))
+        banks_b = layer(1, quant_b)
+        vals_b = [copy_h(1, t, banks_b) for t in range(PACK)]
+
+        pairs16 = [tile([P, 2, CHUNK, 2], BF16, f"pairs16_{c}") for c in range(2)]
+        for t in range(PACK):
+            scatter(1, t, vals_b[t])
+            nc.sync.dma_start(out_rows[t], page[t][:])
+            for c in range(2):
+                nc.scalar.copy(pairs16[c][:, t // 2, :, t % 2], page[t][:, c * CHUNK : (c + 1) * CHUNK])
+        out_words = tile([P, U], I32, "out_words")
+        out_scales = tile([P, U], U8, "out_scales")
+        words_dram = out_1[0].rearrange("p n t -> p (n t)").bitcast(I32)
+        for c in range(2):
+            cols = slice(c * CHUNK, (c + 1) * CHUNK)
+            grouped = tile([P, CHUNK * PACK], BF16, f"out_grouped{c}")
+            nc.vector.tensor_copy(grouped[:].bitcast(F32).rearrange("p (c u) -> p c u", u=2),
+                                  pairs16[c][:].rearrange("p u c e -> p (u c e)").bitcast(F32).rearrange("p (u c) -> p c u", u=2))
+            nc.vector.quantize_mx(out_words[:, cols].bitcast(FP8X4), out_scales[:, cols], grouped[:])
+            nc.sync.dma_start(words_dram[:, cols], out_words[:, cols])
+        for q in range(4):
+            nc.scalar.dma_start(out_2[0, 4 * q : 4 * q + 4, :].bitcast(I32), out_scales[32 * q : 32 * q + 4, :].bitcast(I32))

@@ -21,7 +21,8 @@ P = 128
 PACK = 4
 HALF = S // 2
 LIST_COLS = HALF // 16
-CHUNK = U // 2
+CHUNKS = 4
+CHUNK = U // CHUNKS
 
 
 def tile_picked_swarm2_none_po_kernel(
@@ -51,12 +52,13 @@ def tile_picked_swarm2_none_po_kernel(
             return lst[:, half * LIST_COLS : (half + 1) * LIST_COLS]
 
         pulls_rows = tile([P, P], F32, "pulls_rows")
-        nc.vector.memset(pulls_rows[:], 0.0)
+        nc.gpsimd.memset(pulls_rows[:], 0.0)
         xs = tile([P, T], U8, "xs")
         w1s = tile([P, H], U8, "w1s")
         w2s = tile([P, H], U8, "w2s")
         w3s = tile([P, N], U8, "w3s")
-        for plane in (xs, w2s, w1s, w3s):
+        nc.gpsimd.memset(xs[:].bitcast(I32), 0)
+        for plane in (w2s, w1s, w3s):
             nc.vector.memset(plane[:].bitcast(I32), 0)
         ident = tile([P, P], F32, "ident")
         make_identity(nc, ident[:])
@@ -68,30 +70,25 @@ def tile_picked_swarm2_none_po_kernel(
         n1_l = load_list(n1, "n1_l")
         nc.sync.dma_start(bt[0][:], best_rows[0])
         n2_l = load_list(n2, "n2_l")
-        for t in range(1, PACK):
-            nc.sync.dma_start(bt[t][:], best_rows[t])
+        nc.sync.dma_start(pulls_rows[0:4, :], ra[0:1, :].rearrange("o (b c) -> (o b) c", b=4))
+        nc.sync.dma_start(pulls_rows[4:8, :], rb[0:1, :].rearrange("o (b c) -> (o b) c", b=4))
+        nc.sync.dma_start(bt[1][:], best_rows[1])
+        nc.sync.dma_start(bt[2][:], best_rows[2])
         xw = tile([P, T], I32, "xw")
         nc.sync.dma_start(xw[:], x_words[0].rearrange("p n t -> p (n t)").bitcast(I32))
         two_l = load_list(two, "two_l")
         offs_l = load_list(offs, "offs_l")
-        nc.scalar.dma_start(pulls_rows[0:4, :], ra[0:1, :].rearrange("o (b c) -> (o b) c", b=4))
-        nc.scalar.dma_start(pulls_rows[4:8, :], rb[0:1, :].rearrange("o (b c) -> (o b) c", b=4))
-        load_scales(nc.scalar, xs, x_scales)
+        slot_l = load_list(slot, "slot_l")
+        gain = tile([P, PACK], F32, "gain")
+        nc.sync.dma_start(gain[:], gn.rearrange("(p t) o -> p (t o)", t=PACK))
+        load_scales(nc.sync, xs, x_scales)
+        nc.sync.dma_start(bt[3][:], best_rows[3])
         w1w = tile([P, 2 * H], U8, "w1w")
         w2w = tile([P, 2 * H], U8, "w2w")
         w3w = tile([P, 2 * N], U8, "w3w")
-        nc.sync.dma_start(w2w[:].bitcast(I32), w2_words[0].bitcast(I32))
-        nc.sync.dma_start(w1w[:].bitcast(I32), w1_words[0].bitcast(I32))
-        load_scales(nc.scalar, w2s, w2_scales)
-        load_scales(nc.scalar, w1s, w1_scales)
-        gain = tile([P, PACK], F32, "gain")
-        nc.sync.dma_start(gain[:], gn.rearrange("(p t) o -> p (t o)", t=PACK))
-        nc.sync.dma_start(w3w[:].bitcast(I32), w3_words[0].bitcast(I32))
-        load_scales(nc.sync, w3s, w3_scales)
-        slot_l = load_list(slot, "slot_l")
-        page = [tile([P, U], F32, f"page{t}") for t in range(PACK)]
-        for t in range(PACK):
-            nc.sync.dma_start(page[t][:], mem_rows[t])
+        for words, scales, src_words, src_scales in ((w2w, w2s, w2_words, w2_scales), (w1w, w1s, w1_words, w1_scales), (w3w, w3s, w3_words, w3_scales)):
+            nc.sync.dma_start(words[:].bitcast(I32), src_words[0].bitcast(I32))
+            load_scales(nc.sync, scales, src_scales)
 
         pulls_ps = ring.tile([P, S], F32, name="pulls_ps", tag="ring")
         nc.tensor.transpose(pulls_ps[:, 0:P], pulls_rows[:], ident[:])
@@ -121,8 +118,8 @@ def tile_picked_swarm2_none_po_kernel(
             nc.vector.tensor_tensor(top[:], pair[:, 0, :], pair[:, 1, :], ALU.max)
             return top
 
-        def neighbour_term(half, t, top, pool, tag):
-            ps = pool.tile([P, 2, HALF], F32, name=f"topT{half}{t}", tag=tag)
+        def neighbour_term(half, t, top):
+            ps = ring.tile([P, 2, HALF], F32, name=f"topT{half}{t}", tag="ring")
             term = tile([P, 2, P], F32, f"top_term{half}{t}")
             for b in range(2):
                 nc.tensor.transpose(ps[:, 0, b * P : (b + 1) * P], top[:, b * P : (b + 1) * P], ident[:])
@@ -132,12 +129,17 @@ def tile_picked_swarm2_none_po_kernel(
             for b in range(2):
                 add_term(term[:, b, :], 2 * half + b, t)
 
-        def best_term(jb):
-            ps = ring.tile([P, S], F32, name=f"bestT{jb}", tag="ring")
-            for t in range(PACK):
-                nc.tensor.transpose(ps[:, t * P : (t + 1) * P], bt[t][:, jb * P : (jb + 1) * P], ident[:])
-            term = tile([P, PACK, P], F32, f"best_term{jb}")
-            nc.scalar.activation(term[:].rearrange("j t p -> j (t p)"), ps[:], COPY, scale=pulls[:, jb : jb + 1])
+        def best_term(t):
+            ps = ring.tile([P, S], F32, name=f"bestT{t}", tag="ring")
+            term = tile([P, 4, P], F32, f"best_term{t}")
+            for jb in range(4):
+                nc.tensor.transpose(ps[:, jb * P : (jb + 1) * P], bt[t][:, jb * P : (jb + 1) * P], ident[:])
+            for jb in range(4):
+                nc.scalar.activation(term[:, jb, :], ps[:, jb * P : (jb + 1) * P], COPY, scale=pulls[:, jb : jb + 1])
+            for jb in range(4):
+                add_term(term[:, jb, :], jb, t)
+
+        def add_rows(term, jb):
             for t in range(PACK):
                 add_term(term[:, t, :], jb, t)
 
@@ -148,22 +150,28 @@ def tile_picked_swarm2_none_po_kernel(
             nc.vector.tensor_copy(scales[:], xs[:].indirect(half_of(lst, half)))
             return words, scales
 
-        def product_term(picked, ww, ws, name, jb, scale):
+        def product(picked, ww, ws, name, jb):
             words, scales = picked
             cols = slice((jb % 2) * P, (jb % 2 + 1) * P)
             ps = ring.tile([P, S], F32, name=f"{name}T{jb}", tag="ring")
             nc.tensor.matmul_mx(ps[:], lhsT=words[:, cols].bitcast(FP8X4), lhsT_scale=scales[:, cols],
                                 rhs=ww[:].bitcast(FP4X4), rhs_scale=ws[:], start=True, stop=True)
+            return ps
+
+        def product_term(ps, name, jb, scale):
             term = tile([P, PACK, P], F32, f"{name}_term{jb}")
             nc.scalar.activation(term[:], ps[:].rearrange("j (p t) -> j t p", t=PACK), COPY, scale=scale)
-            for t in range(PACK):
-                add_term(term[:, t, :], jb, t)
+            add_rows(term, jb)
 
-        def product_terms(half, picked_two, picked_offs):
-            for jb in (2 * half, 2 * half + 1):
-                product_term(picked_two, w2w, w2s, "c", jb, 0.75)
-            for jb in (2 * half, 2 * half + 1):
-                product_term(picked_offs, w1w, w1s, "y", jb, neg_sum[:, jb : jb + 1])
+        def speed_terms(half, picked):
+            blocks = (2 * half, 2 * half + 1)
+            for jb, ps in [(jb, product(picked, w2w, w2s, "c", jb)) for jb in blocks]:
+                product_term(ps, "c", jb, 0.75)
+
+        def place_terms(half, picked):
+            blocks = (2 * half, 2 * half + 1)
+            for jb, ps in [(jb, product(picked, w1w, w1s, "y", jb)) for jb in blocks]:
+                product_term(ps, "y", jb, neg_sum[:, jb : jb + 1])
 
         def round_z(half):
             planes = tile([P, PACK, HALF], BF16, f"z_planes{half}")
@@ -179,11 +187,11 @@ def tile_picked_swarm2_none_po_kernel(
             nc.vector.quantize_mx(words[:].bitcast(FP8X4), scales[:], grouped[:].rearrange("p c t -> p (c t)"))
             return words, scales
 
-        def layer(half, quantized):
+        def layer(half, quantized, pool, tags):
             words, scales = quantized
             banks = []
             for u in range(2):
-                ps = ring.tile([P, S], F32, name=f"h{half}{u}", tag="ring")
+                ps = pool.tile([P, S], F32, name=f"h{half}{u}", tag=tags[u])
                 for t in (2 * u, 2 * u + 1):
                     nc.tensor.matmul_mx(ps[:, (t % 2) * HALF : (t % 2 + 1) * HALF],
                                         lhsT=w3w_d[:, t * 2 * P : (t + 1) * 2 * P].bitcast(FP4X4), lhsT_scale=w3s_d[:, t * P : (t + 1) * P],
@@ -199,69 +207,67 @@ def tile_picked_swarm2_none_po_kernel(
         def scatter(half, t, vals):
             nc.vector.tensor_copy(page[t][:].indirect(half_of(slot_l, half)), vals[:])
 
-        tops = []
-        pairs = [neighbour_gathers(0, 0, "pair00")]
-        for t in range(1, PACK):
-            pairs.append(neighbour_gathers(0, t, f"pair0{t}"))
-            tops.append(neighbour_max(0, t - 1, pairs[t - 1]))
+        tops = [neighbour_max(0, t, neighbour_gathers(0, t, f"pair0{t}")) for t in range(3)]
         two_a = pick(two_l, "two", 0)
-        tops.append(neighbour_max(0, PACK - 1, pairs[PACK - 1]))
         offs_a = pick(offs_l, "offs", 0)
-        for jb in range(2):
-            best_term(jb)
-        for t in range(PACK):
-            neighbour_term(0, t, tops[t], ring, "ring")
-        product_terms(0, two_a, offs_a)
+        tops.append(neighbour_max(0, 3, neighbour_gathers(0, 3, "pair03")))
+        for t in range(3):
+            best_term(t)
+            neighbour_term(0, t, tops[t])
+        best_term(3)
+        speed_terms(0, two_a)
+        neighbour_term(0, 3, tops[3])
+        place_terms(0, offs_a)
         grouped_a = round_z(0)
+
+        page = [tile([P, U], F32, f"page{t}", f"pair0{t}") for t in range(PACK)]
+        for t in range(PACK):
+            nc.sync.dma_start(page[t][:], mem_rows[t])
 
         w3w_d = tile([P, 2 * N], U8, "w3w_d")
         w3s_d = tile([P, N], U8, "w3s_d")
         nc.vector.tensor_copy(w3w_d[:].rearrange("k (t m b) -> k t m b", t=PACK, b=2), w3w[:].rearrange("k (m t b) -> k t m b", t=PACK, b=2))
         nc.vector.tensor_copy(w3s_d[:].rearrange("k (t m) -> k t m", t=PACK), w3s[:].rearrange("k (m t) -> k t m", t=PACK))
 
+        banks_a = layer(0, quantize_z(0, grouped_a), acc, ("z00", "z01"))
+        vals_a = [copy_h(0, t, banks_a) for t in range(3)]
+
         two_b = pick(two_l, "two", 1)
         offs_b = pick(offs_l, "offs", 1)
-        for jb in range(2, 4):
-            best_term(jb)
-        product_terms(1, two_b, offs_b)
-        pair0 = neighbour_gathers(1, 0, "two_words0")
-        pair1 = neighbour_gathers(1, 1, "offs_words0")
-        top0 = neighbour_max(1, 0, pair0)
-        pair2 = neighbour_gathers(1, 2, "two_words0")
-        top1 = neighbour_max(1, 1, pair1)
-        quant_a = quantize_z(0, grouped_a)
-        top2 = neighbour_max(1, 2, pair2)
-        for t, top in enumerate((top0, top1, top2)):
-            neighbour_term(1, t, top, acc, f"z0{t % 2}")
-        banks_a = layer(0, quant_a)
-        pair3 = neighbour_gathers(1, 3, "z_grouped0")
-        top3 = neighbour_max(1, 3, pair3)
-        vals_a = [copy_h(0, 0, banks_a)]
-        neighbour_term(1, 3, top3, acc, "z01")
+        speed_terms(1, two_b)
+        place_terms(1, offs_b)
+        for t, tag in enumerate(("two_words0", "offs_words0", "two_words0")):
+            neighbour_term(1, t, neighbour_max(1, t, neighbour_gathers(1, t, tag)))
+        top3 = neighbour_max(1, 3, neighbour_gathers(1, 3, "z_planes0"))
+        neighbour_term(1, 3, top3)
         grouped_b = round_z(1)
-        vals_a.extend(copy_h(0, t, banks_a) for t in (1, 2))
         for t in range(3):
             scatter(0, t, vals_a[t])
         quant_b = quantize_z(1, grouped_b)
-        scatter(0, 3, copy_h(0, 3, banks_a, "z_grouped1"))
-        banks_b = layer(1, quant_b)
+        scatter(0, 3, copy_h(0, 3, banks_a, "z_planes1"))
+        banks_b = layer(1, quant_b, acc, ("z10", "z11"))
         vals_b = [copy_h(1, t, banks_b) for t in range(PACK)]
 
-        pairs16 = [tile([P, 2, CHUNK, 2], BF16, f"pairs16_{c}") for c in range(2)]
+        pairs16 = tile([P, PACK * U], BF16, "pairs16")
+        pair_slots = pairs16[:].rearrange("p (k u c e) -> p k u c e", k=CHUNKS, u=2, e=2)
         for t in range(PACK):
             scatter(1, t, vals_b[t])
             nc.sync.dma_start(out_rows[t], page[t][:])
-            for c in range(2):
-                nc.scalar.copy(pairs16[c][:, t // 2, :, t % 2], page[t][:, c * CHUNK : (c + 1) * CHUNK])
+            if t < PACK - 1:
+                nc.scalar.copy(pair_slots[:, :, t // 2, :, t % 2], page[t][:].rearrange("p (k c) -> p k c", k=CHUNKS))
+        for c in range(CHUNKS):
+            nc.scalar.copy(pair_slots[:, c, 1, :, 1], page[PACK - 1][:, c * CHUNK : (c + 1) * CHUNK])
         out_words = tile([P, U], I32, "out_words")
         out_scales = tile([P, U], U8, "out_scales")
         words_dram = out_1[0].rearrange("p n t -> p (n t)").bitcast(I32)
-        for c in range(2):
-            cols = slice(c * CHUNK, (c + 1) * CHUNK)
-            grouped = tile([P, CHUNK * PACK], BF16, f"out_grouped{c}")
-            nc.vector.tensor_copy(grouped[:].bitcast(F32).rearrange("p (c u) -> p c u", u=2),
-                                  pairs16[c][:].rearrange("p u c e -> p (u c e)").bitcast(F32).rearrange("p (u c) -> p c u", u=2))
-            nc.vector.quantize_mx(out_words[:, cols].bitcast(FP8X4), out_scales[:, cols], grouped[:])
-            nc.sync.dma_start(words_dram[:, cols], out_words[:, cols])
+        grouped = [tile([P, CHUNK * PACK], BF16, f"out_grouped{c}") for c in range(CHUNKS)]
+        for step in range(CHUNKS + 1):
+            if step < CHUNKS:
+                nc.vector.tensor_copy(grouped[step][:].bitcast(F32).rearrange("p (c u) -> p c u", u=2),
+                                      pairs16[:, step * PACK * CHUNK : (step + 1) * PACK * CHUNK].bitcast(F32).rearrange("p (u c) -> p c u", u=2))
+            if step > 0:
+                cols = slice((step - 1) * CHUNK, step * CHUNK)
+                nc.vector.quantize_mx(out_words[:, cols].bitcast(FP8X4), out_scales[:, cols], grouped[step - 1][:])
+                nc.sync.dma_start(words_dram[:, cols], out_words[:, cols])
         for q in range(4):
             nc.scalar.dma_start(out_2[0, 4 * q : 4 * q + 4, :].bitcast(I32), out_scales[32 * q : 32 * q + 4, :].bitcast(I32))

@@ -90,6 +90,14 @@ def tile_picked_swarm2_none_po_kernel(
             nc.sync.dma_start(words[:].bitcast(I32), src_words[0].bitcast(I32))
             load_scales(nc.sync, scales, src_scales)
 
+        def turn_best(t):
+            ps = ring.tile([P, S], F32, name=f"bestT{t}", tag="ring")
+            for jb in range(4):
+                nc.tensor.transpose(ps[:, jb * P : (jb + 1) * P], bt[t][:, jb * P : (jb + 1) * P], ident[:])
+            return ps
+
+        turned = [turn_best(t) for t in range(3)]
+
         pulls_ps = ring.tile([P, S], F32, name="pulls_ps", tag="ring")
         nc.tensor.transpose(pulls_ps[:, 0:P], pulls_rows[:], ident[:])
         pulls = tile([P, 8], F32, "pulls")
@@ -129,11 +137,8 @@ def tile_picked_swarm2_none_po_kernel(
             for b in range(2):
                 add_term(term[:, b, :], 2 * half + b, t)
 
-        def best_term(t):
-            ps = ring.tile([P, S], F32, name=f"bestT{t}", tag="ring")
+        def best_term(t, ps):
             term = tile([P, 4, P], F32, f"best_term{t}")
-            for jb in range(4):
-                nc.tensor.transpose(ps[:, jb * P : (jb + 1) * P], bt[t][:, jb * P : (jb + 1) * P], ident[:])
             for jb in range(4):
                 nc.scalar.activation(term[:, jb, :], ps[:, jb * P : (jb + 1) * P], COPY, scale=pulls[:, jb : jb + 1])
             for jb in range(4):
@@ -212,12 +217,17 @@ def tile_picked_swarm2_none_po_kernel(
         offs_a = pick(offs_l, "offs", 0)
         tops.append(neighbour_max(0, 3, neighbour_gathers(0, 3, "pair03")))
         for t in range(3):
-            best_term(t)
+            best_term(t, turned[t])
+        for t in range(3):
             neighbour_term(0, t, tops[t])
-        best_term(3)
-        speed_terms(0, two_a)
+        best_term(3, turn_best(3))
+        speeds = [product(two_a, w2w, w2s, "c", jb) for jb in range(2)]
+        places = [product(offs_a, w1w, w1s, "y", jb) for jb in range(2)]
+        for jb in range(2):
+            product_term(speeds[jb], "c", jb, 0.75)
         neighbour_term(0, 3, tops[3])
-        place_terms(0, offs_a)
+        for jb in range(2):
+            product_term(places[jb], "y", jb, neg_sum[:, jb : jb + 1])
         grouped_a = round_z(0)
 
         page = [tile([P, U], F32, f"page{t}", f"pair0{t}") for t in range(PACK)]
@@ -226,8 +236,9 @@ def tile_picked_swarm2_none_po_kernel(
 
         w3w_d = tile([P, 2 * N], U8, "w3w_d")
         w3s_d = tile([P, N], U8, "w3s_d")
-        nc.vector.tensor_copy(w3w_d[:].rearrange("k (t m b) -> k t m b", t=PACK, b=2), w3w[:].rearrange("k (m t b) -> k t m b", t=PACK, b=2))
-        nc.vector.tensor_copy(w3s_d[:].rearrange("k (t m) -> k t m", t=PACK), w3s[:].rearrange("k (m t) -> k t m", t=PACK))
+        for t in range(PACK):
+            nc.gpsimd.tensor_copy(w3w_d[:].rearrange("k (t m b) -> k t m b", t=PACK, b=2)[:, t], w3w[:].rearrange("k (m t b) -> k t m b", t=PACK, b=2)[:, t])
+            nc.gpsimd.tensor_copy(w3s_d[:].rearrange("k (t m) -> k t m", t=PACK)[:, t], w3s[:].rearrange("k (m t) -> k t m", t=PACK)[:, t])
 
         banks_a = layer(0, quantize_z(0, grouped_a), acc, ("z00", "z01"))
         vals_a = [copy_h(0, t, banks_a) for t in range(3)]
@@ -236,8 +247,9 @@ def tile_picked_swarm2_none_po_kernel(
         offs_b = pick(offs_l, "offs", 1)
         speed_terms(1, two_b)
         place_terms(1, offs_b)
-        for t, tag in enumerate(("two_words0", "offs_words0", "two_words0")):
-            neighbour_term(1, t, neighbour_max(1, t, neighbour_gathers(1, t, tag)))
+        pairs_b = [neighbour_gathers(1, t, tag) for t, tag in enumerate(("two_words0", "two_scales0", "offs_words0"))]
+        for t in range(3):
+            neighbour_term(1, t, neighbour_max(1, t, pairs_b[t]))
         top3 = neighbour_max(1, 3, neighbour_gathers(1, 3, "z_planes0"))
         neighbour_term(1, 3, top3)
         grouped_b = round_z(1)

from contextlib import ExitStack

import concourse.mybir as mybir
from concourse.masks import make_identity

K, T, S, N, H, U = 512, 2048, 512, 512, 512, 1024
FLOPS = 3 * 2 * 512 * 512 * 512

F32 = mybir.dt.float32
BF16 = mybir.dt.bfloat16
I32 = mybir.dt.int32
U32 = mybir.dt.uint32
U16 = mybir.dt.uint16
U8 = mybir.dt.uint8
FP8X4 = mybir.dt.float8_e4m3fn_x4
FP4X4 = mybir.dt.float4_e2m1fn_x4
COPY = mybir.ActivationFunctionType.Copy
ALU = mybir.AluOpType

P = 128
PACK = 4
HALF = S // 2
LIST_COLS = HALF // 16
CHUNKS = 4
CHUNK = U // CHUNKS


def tile_picked_swarm2_none_po_kernel(
    tc, x_words, x_scales, w1_words, w1_scales, w2_words, w2_scales, best, ra, rb, gn,
    w3_words, w3_scales, mem, offs, two, n1, n2, slot, out_0, out_1, out_2,
):
    nc = tc.nc
    with ExitStack() as ctx:
        lists = ctx.enter_context(tc.tile_pool(name="lists", bufs=1))
        sb = ctx.enter_context(tc.tile_pool(name="sb", bufs=1))
        acc = ctx.enter_context(tc.psum_pool(name="acc", bufs=1))
        ring = ctx.enter_context(tc.psum_pool(name="ring", bufs=4))

        def tile(shape, dtype, name, tag=None):
            return sb.tile(shape, dtype, name=name, tag=tag or name, align_bytes=64)

        def load_list(src, name):
            dst = lists.tile([P, S // 16], U16, name=name)
            nc.sync.dma_start(dst[:], src)
            return dst

        def load_scales(queue, dst, src):
            for q in range(4):
                queue.dma_start(dst[32 * q : 32 * q + 4, :].bitcast(I32), src[0, 4 * q : 4 * q + 4, :].bitcast(I32))

        def half_of(lst, half):
            return lst[:, half * LIST_COLS : (half + 1) * LIST_COLS]

        pulls_rows = tile([P, P], F32, "pulls_rows")
        nc.gpsimd.memset(pulls_rows[:], 0.0)
        xs = tile([P, T], U8, "xs")
        w1s = tile([P, H], U8, "w1s")
        w2s = tile([P, H], U8, "w2s")
        w3s = tile([P, N], U8, "w3s")
        nc.gpsimd.memset(xs[:].bitcast(I32), 0)
        for plane in (w2s, w1s, w3s):
            nc.vector.memset(plane[:].bitcast(I32), 0)
        ident = tile([P, P], F32, "ident")
        make_identity(nc, ident[:])

        best_rows = best.rearrange("(p t) j -> t p j", t=PACK)
        mem_rows = mem.rearrange("(p t) c -> t p c", t=PACK)
        out_rows = out_0.rearrange("(p t) c -> t p c", t=PACK)
        bt = [tile([P, S], F32, f"best{t}") for t in range(PACK)]
        n1_l = load_list(n1, "n1_l")
        nc.sync.dma_start(bt[0][:], best_rows[0])
        n2_l = load_list(n2, "n2_l")
        nc.sync.dma_start(pulls_rows[0:4, :], ra[0:1, :].rearrange("o (b c) -> (o b) c", b=4))
        nc.sync.dma_start(pulls_rows[4:8, :], rb[0:1, :].rearrange("o (b c) -> (o b) c", b=4))
        nc.sync.dma_start(bt[1][:], best_rows[1])
        nc.sync.dma_start(bt[2][:], best_rows[2])
        xw = tile([P, T], I32, "xw")
        nc.sync.dma_start(xw[:], x_words[0].rearrange("p n t -> p (n t)").bitcast(I32))
        two_l = load_list(two, "two_l")
        offs_l = load_list(offs, "offs_l")
        slot_l = load_list(slot, "slot_l")
        gain = tile([P, PACK], F32, "gain")
        nc.sync.dma_start(gain[:], gn.rearrange("(p t) o -> p (t o)", t=PACK))
        load_scales(nc.sync, xs, x_scales)
        nc.sync.dma_start(bt[3][:], best_rows[3])
        w1w = tile([P, 2 * H], U8, "w1w")
        w2w = tile([P, 2 * H], U8, "w2w")
        w3w = tile([P, 2 * N], U8, "w3w")
        for words, scales, src_words, src_scales in ((w2w, w2s, w2_words, w2_scales), (w1w, w1s, w1_words, w1_scales), (w3w, w3s, w3_words, w3_scales)):
            nc.sync.dma_start(words[:].bitcast(I32), src_words[0].bitcast(I32))
            load_scales(nc.sync, scales, src_scales)

        def turn_best(t):
            ps = ring.tile([P, S], F32, name=f"bestT{t}", tag="ring")
            for jb in range(4):
                nc.tensor.transpose(ps[:, jb * P : (jb + 1) * P], bt[t][:, jb * P : (jb + 1) * P], ident[:])
            return ps

        turned = [turn_best(t) for t in range(3)]

        pulls_ps = ring.tile([P, S], F32, name="pulls_ps", tag="ring")
        nc.tensor.transpose(pulls_ps[:, 0:P], pulls_rows[:], ident[:])
        pulls = tile([P, 8], F32, "pulls")
        nc.scalar.copy(pulls[:], pulls_ps[:, 0:8])
        neg_sum = tile([P, 4], F32, "neg_sum")
        nc.vector.scalar_tensor_tensor(neg_sum[:], pulls[:, 0:4], -1.0, pulls[:, 4:8], ALU.mult, ALU.subtract)

        zsum = [[acc.tile([P, 2, HALF], F32, name=f"zsum{h}{u}", tag=f"z{h}{u}") for u in range(2)] for h in range(2)]
        added = {}

        def add_term(term, jb, t):
            h, u = jb // 2, t // 2
            count = added.get((h, u), 0)
            added[(h, u)] = count + 1
            c0 = (jb % 2) * P
            nc.tensor.matmul(zsum[h][u][:, t % 2, c0 : c0 + P], term, ident[:], start=(count == 0), stop=(count == 15), is_transpose=True)

        def neighbour_gathers(half, t, tag):
            pair = tile([P, 2, HALF], F32, f"pair{half}{t}", tag)
            nc.vector.tensor_copy(pair[:, 0, :], bt[t][:].indirect(half_of(n1_l, half)))
            nc.vector.tensor_copy(pair[:, 1, :], bt[t][:].indirect(half_of(n2_l, half)))
            return pair

        def neighbour_max(half, t, pair):
            top = tile([P, HALF], F32, f"top{half}{t}")
            nc.vector.tensor_tensor(top[:], pair[:, 0, :], pair[:, 1, :], ALU.max)
            return top

        def neighbour_term(half, t, top):
            ps = ring.tile([P, 2, HALF], F32, name=f"topT{half}{t}", tag="ring")
            term = tile([P, 2, P], F32, f"top_term{half}{t}")
            for b in range(2):
                nc.tensor.transpose(ps[:, 0, b * P : (b + 1) * P], top[:, b * P : (b + 1) * P], ident[:])
            for b in range(2):
                jb = 2 * half + b
                nc.scalar.activation(term[:, b, :], ps[:, 0, b * P : (b + 1) * P], COPY, scale=pulls[:, 4 + jb : 5 + jb])
            for b in range(2):
                add_term(term[:, b, :], 2 * half + b, t)

        def best_term(t, ps):
            term = tile([P, 4, P], F32, f"best_term{t}")
            for jb in range(4):
                nc.scalar.activation(term[:, jb, :], ps[:, jb * P : (jb + 1) * P], COPY, scale=pulls[:, jb : jb + 1])
            for jb in range(4):
                add_term(term[:, jb, :], jb, t)

        def add_rows(term, jb):
            for t in range(PACK):
                add_term(term[:, t, :], jb, t)

        def pick(lst, name, half):
            words = tile([P, HALF], I32, f"{name}_words{half}")
            scales = tile([P, HALF], U8, f"{name}_scales{half}")
            nc.vector.tensor_copy(words[:].bitcast(U32), xw[:].bitcast(U32).indirect(half_of(lst, half)))
            nc.vector.tensor_copy(scales[:], xs[:].indirect(half_of(lst, half)))
            return words, scales

        def product(picked, ww, ws, name, jb):
            words, scales = picked
            cols = slice((jb % 2) * P, (jb % 2 + 1) * P)
            ps = ring.tile([P, S], F32, name=f"{name}T{jb}", tag="ring")
            nc.tensor.matmul_mx(ps[:], lhsT=words[:, cols].bitcast(FP8X4), lhsT_scale=scales[:, cols],
                                rhs=ww[:].bitcast(FP4X4), rhs_scale=ws[:], start=True, stop=True)
            return ps

        def product_term(ps, name, jb, scale):
            term = tile([P, PACK, P], F32, f"{name}_term{jb}")
            nc.scalar.activation(term[:], ps[:].rearrange("j (p t) -> j t p", t=PACK), COPY, scale=scale)
            add_rows(term, jb)

        def speed_terms(half, picked):
            blocks = (2 * half, 2 * half + 1)
            for jb, ps in [(jb, product(picked, w2w, w2s, "c", jb)) for jb in blocks]:
                product_term(ps, "c", jb, 0.75)

        def place_terms(half, picked):
            blocks = (2 * half, 2 * half + 1)
            for jb, ps in [(jb, product(picked, w1w, w1s, "y", jb)) for jb in blocks]:
                product_term(ps, "y", jb, neg_sum[:, jb : jb + 1])

        def round_z(half):
            planes = tile([P, PACK, HALF], BF16, f"z_planes{half}")
            for t in range(PACK):
                nc.scalar.activation(planes[:, t, :], zsum[half][t // 2][:, t % 2, :], COPY, scale=gain[:, t : t + 1])
            grouped = tile([P, HALF, PACK], BF16, f"z_grouped{half}")
            nc.scalar.copy(grouped[:].rearrange("p (c i) t -> p c t i", i=4), planes[:].rearrange("p t (c i) -> p c t i", i=4))
            return grouped

        def quantize_z(half, grouped):
            words = tile([P, HALF], I32, f"z_words{half}")
            scales = tile([P, HALF], U8, f"z_scales{half}")
            nc.vector.quantize_mx(words[:].bitcast(FP8X4), scales[:], grouped[:].rearrange("p c t -> p (c t)"))
            return words, scales

        def layer(half, quantized, pool, tags):
            words, scales = quantized
            banks = []
            for u in range(2):
                ps = pool.tile([P, S], F32, name=f"h{half}{u}", tag=tags[u])
                for t in (2 * u, 2 * u + 1):
                    nc.tensor.matmul_mx(ps[:, (t % 2) * HALF : (t % 2 + 1) * HALF],
                                        lhsT=w3w_d[:, t * 2 * P : (t + 1) * 2 * P].bitcast(FP4X4), lhsT_scale=w3s_d[:, t * P : (t + 1) * P],
                                        rhs=words[:].bitcast(FP8X4), rhs_scale=scales[:], start=True, stop=True)
                banks.append(ps)
            return banks

        def copy_h(half, t, banks, tag=None):
            vals = tile([P, HALF], F32, f"h_vals{half}{t}", tag)
            nc.scalar.copy(vals[:], banks[t // 2][:, (t % 2) * HALF : (t % 2 + 1) * HALF])
            return vals

        def scatter(half, t, vals):
            nc.vector.tensor_copy(page[t][:].indirect(half_of(slot_l, half)), vals[:])

        tops = [neighbour_max(0, t, neighbour_gathers(0, t, f"pair0{t}")) for t in range(3)]
        two_a = pick(two_l, "two", 0)
        offs_a = pick(offs_l, "offs", 0)
        tops.append(neighbour_max(0, 3, neighbour_gathers(0, 3, "pair03")))
        for t in range(3):
            best_term(t, turned[t])
        for t in range(3):
            neighbour_term(0, t, tops[t])
        best_term(3, turn_best(3))
        speeds = [product(two_a, w2w, w2s, "c", jb) for jb in range(2)]
        places = [product(offs_a, w1w, w1s, "y", jb) for jb in range(2)]
        for jb in range(2):
            product_term(speeds[jb], "c", jb, 0.75)
        neighbour_term(0, 3, tops[3])
        for jb in range(2):
            product_term(places[jb], "y", jb, neg_sum[:, jb : jb + 1])
        grouped_a = round_z(0)

        page = [tile([P, U], F32, f"page{t}", f"pair0{t}") for t in range(PACK)]
        for t in range(PACK):
            nc.sync.dma_start(page[t][:], mem_rows[t])

        w3w_d = tile([P, 2 * N], U8, "w3w_d")
        w3s_d = tile([P, N], U8, "w3s_d")
        for t in range(PACK):
            nc.gpsimd.tensor_copy(w3w_d[:].rearrange("k (t m b) -> k t m b", t=PACK, b=2)[:, t], w3w[:].rearrange("k (m t b) -> k t m b", t=PACK, b=2)[:, t])
            nc.gpsimd.tensor_copy(w3s_d[:].rearrange("k (t m) -> k t m", t=PACK)[:, t], w3s[:].rearrange("k (m t) -> k t m", t=PACK)[:, t])

        banks_a = layer(0, quantize_z(0, grouped_a), acc, ("z00", "z01"))
        vals_a = [copy_h(0, t, banks_a) for t in range(3)]

        two_b = pick(two_l, "two", 1)
        offs_b = pick(offs_l, "offs", 1)
        speed_terms(1, two_b)
        place_terms(1, offs_b)
        pairs_b = [neighbour_gathers(1, t, tag) for t, tag in enumerate(("two_words0", "two_scales0", "offs_words0"))]
        for t in range(3):
            neighbour_term(1, t, neighbour_max(1, t, pairs_b[t]))
        top3 = neighbour_max(1, 3, neighbour_gathers(1, 3, "z_planes0"))
        neighbour_term(1, 3, top3)
        grouped_b = round_z(1)
        for t in range(3):
            scatter(0, t, vals_a[t])
        quant_b = quantize_z(1, grouped_b)
        scatter(0, 3, copy_h(0, 3, banks_a, "z_planes1"))
        banks_b = layer(1, quant_b, acc, ("z10", "z11"))
        vals_b = [copy_h(1, t, banks_b) for t in range(PACK)]

        pairs16 = tile([P, PACK * U], BF16, "pairs16")
        pair_slots = pairs16[:].rearrange("p (k u c e) -> p k u c e", k=CHUNKS, u=2, e=2)
        for t in range(PACK):
            scatter(1, t, vals_b[t])
            nc.sync.dma_start(out_rows[t], page[t][:])
            if t < PACK - 1:
                nc.scalar.copy(pair_slots[:, :, t // 2, :, t % 2], page[t][:].rearrange("p (k c) -> p k c", k=CHUNKS))
        for c in range(CHUNKS):
            nc.scalar.copy(pair_slots[:, c, 1, :, 1], page[PACK - 1][:, c * CHUNK : (c + 1) * CHUNK])
        out_words = tile([P, U], I32, "out_words")
        out_scales = tile([P, U], U8, "out_scales")
        words_dram = out_1[0].rearrange("p n t -> p (n t)").bitcast(I32)
        grouped = [tile([P, CHUNK * PACK], BF16, f"out_grouped{c}") for c in range(CHUNKS)]
        for step in range(CHUNKS + 1):
            if step < CHUNKS:
                nc.vector.tensor_copy(grouped[step][:].bitcast(F32).rearrange("p (c u) -> p c u", u=2),
                                      pairs16[:, step * PACK * CHUNK : (step + 1) * PACK * CHUNK].bitcast(F32).rearrange("p (u c) -> p c u", u=2))
            if step > 0:
                cols = slice((step - 1) * CHUNK, step * CHUNK)
                nc.vector.quantize_mx(out_words[:, cols].bitcast(FP8X4), out_scales[:, cols], grouped[step - 1][:])
                nc.sync.dma_start(words_dram[:, cols], out_words[:, cols])
        for q in range(4):
            nc.scalar.dma_start(out_2[0, 4 * q : 4 * q + 4, :].bitcast(I32), out_scales[32 * q : 32 * q + 4, :].bitcast(I32))
